import numpy as np
import ml_dtypes


def mxq(x, axis, fmt="e4m3"):
    dtype, down = {"e4m3": (ml_dtypes.float8_e4m3fn, 7), "e5m2": (ml_dtypes.float8_e5m2, 14)}[fmt]
    v = np.moveaxis(np.asarray(x, np.float32).astype(ml_dtypes.bfloat16).astype(np.float64), axis, -1)
    blocks = v.reshape(v.shape[:-1] + (-1, 32))
    amax = np.abs(blocks).max(-1, keepdims=True)
    byte = np.maximum(np.where(amax > 0, np.frexp(amax)[1] - 1 + 127, 0) - down, 1)
    scale = np.exp2(byte - 127.0)
    codes = (blocks / scale).astype(np.float32).astype(dtype).astype(np.float64)
    return np.moveaxis((codes * scale).reshape(v.shape), -1, axis)


WIDE = False


def mx_kscale(k):
    if not WIDE:
        return np.ones(k)
    levels = np.array([30, -30])
    if k % 512:
        return np.exp2(np.random.permutation(np.resize(levels, k // 32))).repeat(32)
    a = np.empty((k // 512, 16))
    for p in range(k // 512):
        a[p, :8] = np.random.permutation(np.resize(levels, 8))
        for g in range(8):
            far = levels[np.abs(levels - a[p, g]) >= 10]
            a[p, g + 8] = far[np.random.randint(len(far))]
    return np.exp2(a.ravel()).repeat(32)


def f64(x):
    return np.asarray(x).astype(np.float64)


def striped(idx):
    return np.tile(np.asarray(idx).reshape(-1, 16).T, (8, 1)).astype(np.uint16)


def unstriped(offs):
    return offs[:16].T.reshape(-1).astype(np.int64)


def striped8(idx):
    return np.asarray(idx).reshape(8, -1, 16).transpose(0, 2, 1).reshape(128, -1).astype(np.uint16)


def unstriped8(offs):
    return offs.reshape(8, 16, -1).transpose(0, 2, 1).reshape(8, -1).astype(np.int64)


def pick8(x, idx, run):
    r = np.arange(len(x))
    return x[r[:, None], idx[r % (8 * run) // run]]


E2M1 = np.array([0.0, 0.5, 1.0, 1.5, 2.0, 3.0, 4.0, 6.0, -0.0, -0.5, -1.0, -1.5, -2.0, -3.0, -4.0, -6.0])


def pack_weight(w, fmt):
    k, n = w.shape
    w = f64(np.asarray(w, np.float32).astype(ml_dtypes.bfloat16)).reshape(k // 32, 32, n)
    amax = np.abs(w).max(1)
    if fmt == "e4m3":
        byte = np.frexp(amax)[1] - 1 + 127 - 7
    else:
        mant, ex = np.frexp(amax / 6.0)
        byte = np.where(mant > 0.5, ex, ex - 1) + 127
    byte = np.clip(np.where(amax > 0, byte, 1), 1, 254)
    scaled = (w * np.exp2(127.0 - byte)[:, None, :]).reshape(k, n).astype(np.float32)
    by_word = np.ascontiguousarray(scaled.reshape(k // 512, 128, 4, n).transpose(0, 1, 3, 2))
    if fmt == "e4m3":
        words = by_word.astype(ml_dtypes.float8_e4m3fn).view(np.uint8)
    else:
        c = by_word.astype(ml_dtypes.float4_e2m1fn).view(np.uint8) & 0xF
        words = (c[..., 0::2] | (c[..., 1::2] << 4)).reshape(k // 512, 128, 2 * n)
    return np.ascontiguousarray(words), np.ascontiguousarray(byte.astype(np.uint8).reshape(k // 512, 16, n))


def unpack_weight(words, scales, fmt):
    g, _, n = scales.shape
    words = np.ascontiguousarray(words).reshape(g, 128, n, -1)
    if fmt == "e4m3":
        vals = words.view(ml_dtypes.float8_e4m3fn).astype(np.float64)
    else:
        nib = np.empty((g, 128, n, 4), np.uint8)
        nib[..., 0::2] = words & 0xF
        nib[..., 1::2] = words >> 4
        vals = E2M1[nib]
    vals = vals * np.repeat(np.exp2(scales.astype(np.float64) - 127.0), 8, axis=1)[..., None]
    return vals.transpose(0, 1, 3, 2).reshape(g * 512, n)


K, J, N, R, T, V = 512, 512, 256, 256, 1024, 1024


def setup_inputs():
    n = np.random.standard_normal
    idx = np.stack([np.random.permutation(T)[:J] for _ in range(8)])
    idx2 = np.random.permutation(V)[:J]
    fj = mx_kscale(J)
    fk = mx_kscale(K)
    drp = pack_weight(n((K, R)) * 1 / np.sqrt(K) / fk[:, None], "e2m1")
    return {
        "xf": (n((K, T))).astype(np.float32),
        "ra": (np.random.uniform(0.5, 1.5, (1, J)) * fj).astype(np.float32),
        "gt": (n((N, V)) * np.exp(0.5 * n((1, V)))).astype(np.float32),
        "cb": (np.random.uniform(0.5, 1.5, (J, 1)) / fj[:, None]).astype(np.float32),
        "fkr": (np.random.uniform(0.5, 1.5, (1, K)) * fk).astype(np.float32),
        "dr_words": drp[0],
        "dr_scales": drp[1],
        "bn": (np.random.uniform(-12.0, 12.0, (1, N))).astype(np.float32),
        "offs": striped8(idx),
        "offs2": striped(idx2),
    }


def reference(xf, ra, gt, cb, fkr, dr_words, dr_scales, bn, offs, offs2):
    idx = unstriped8(offs)
    idx2 = unstriped(offs2)
    dru = unpack_weight(dr_words, dr_scales, "e2m1")
    us = pick8(f64(xf), idx, 64) * f64(ra)
    ut = us.T
    uj = ut * f64(fkr)
    gr1 = f64(gt)[:, idx2].T
    gj = gr1 / (np.max(np.abs(gr1), axis=1, keepdims=True) + 0.2) * f64(cb)
    ujq = mxq(uj, 0, "e5m2")
    gjq = mxq(gj, 0, "e5m2")
    w = ujq.T @ gjq
    wq = mxq(w, 0, "e5m2")
    v2 = dru.T @ wq
    wv = v2 + f64(bn)
    mn = np.mean(wv, axis=1, keepdims=True)
    dw = wv - mn
    y = dw / (np.mean(np.abs(dw), axis=1, keepdims=True) + 2.0)
    return y

@@ -1,0 +1,243 @@
+from contextlib import ExitStack
+
+import concourse.mybir as mybir
+from concourse.masks import make_identity
+
+K, J, N, R, T, V = 512, 512, 256, 256, 1024, 1024
+FLOPS = 2 * J * K * N + 2 * K * R * N
+
+F32 = mybir.dt.float32
+BF16 = mybir.dt.bfloat16
+I32 = mybir.dt.int32
+U32 = mybir.dt.uint32
+U16 = mybir.dt.uint16
+U8 = mybir.dt.uint8
+E5M2X4 = mybir.dt.float8_e5m2_x4
+E2M1X4 = mybir.dt.float4_e2m1fn_x4
+ALU = mybir.AluOpType
+ACT = mybir.ActivationFunctionType
+AXIS_X = mybir.AxisListType.X
+
+P = 128
+PACK = 4
+HALVES = 2
+LIST_COLS = J // 16
+G_SHARE = [16, 18]
+X_SHARE = [16, 0, 0, 16]
+X_PARTS = [1, 1, 1, 2]
+
+
+def tile_list_directions_headpicks_sized_spread_kernel(
+    tc, xf, ra, gt, cb, fkr, dr_words, dr_scales, bn, offs, offs2, out
+):
+    nc = tc.nc
+    with ExitStack() as ctx:
+        sb = ctx.enter_context(tc.tile_pool(name="sb", bufs=1))
+        ps = ctx.enter_context(tc.psum_pool(name="ps", bufs=1))
+
+        x_list = sb.tile([P, LIST_COLS], U16, name="x_list")
+        g_list = sb.tile([P, LIST_COLS], U16, name="g_list")
+        g_tab = [sb.tile([P, V], F32, name=f"g_tab{a}") for a in range(HALVES)]
+        x_tab = [sb.tile([P, T], F32, name=f"x_tab{t}") for t in range(PACK)]
+        ra4 = sb.tile([P, PACK], F32, name="ra4")
+        fk4 = sb.tile([P, PACK], F32, name="fk4")
+        cb4 = sb.tile([P, PACK], F32, name="cb4")
+        bn2 = sb.tile([P, HALVES], F32, name="bn2")
+        dr_w = sb.tile([P, 2 * R], U8, name="dr_w", align_bytes=64)
+        dr_s = sb.tile([P, R], U8, name="dr_s", align_bytes=64)
+        ident = sb.tile([P, P], F32, name="ident")
+
+        x_rows = xf.rearrange("(p t) c -> t p c", t=PACK)
+        nc.sync.dma_start(out=g_tab[0][:], in_=gt[0:P, :])
+        nc.sync.dma_start(g_list[:], offs2)
+        nc.sync.dma_start(x_list[:], offs)
+        nc.scalar.dma_start(out=ra4[:], in_=ra.rearrange("o (q s) -> q (o s)", s=PACK))
+        nc.scalar.dma_start(out=fk4[:], in_=fkr.rearrange("o (p t) -> p (o t)", t=PACK))
+        nc.sync.dma_start(out=x_tab[0][:], in_=x_rows[0])
+        nc.sync.dma_start(out=g_tab[1][:], in_=gt[P : 2 * P, :])
+        nc.scalar.dma_start(out=bn2[:], in_=bn.rearrange("o (p a) -> p (o a)", a=HALVES))
+        for t in range(1, PACK):
+            nc.sync.dma_start(out=x_tab[t][:], in_=x_rows[t])
+        nc.sync.dma_start(out=cb4[:], in_=cb.rearrange("(q s) o -> q (s o)", s=PACK))
+        make_identity(nc, ident[:])
+        nc.gpsimd.memset(dr_s[:].bitcast(I32), 0)
+        nc.sync.dma_start(out=dr_w[:].bitcast(I32), in_=dr_words[0].bitcast(I32))
+        for q in range(4):
+            nc.sync.dma_start(
+                out=dr_s[32 * q : 32 * q + 4, :].bitcast(I32),
+                in_=dr_scales[0, 4 * q : 4 * q + 4, :].bitcast(I32),
+            )
+
+        def gather(dst, table, offsets, vector_cols):
+            if vector_cols > 0:
+                nc.vector.tensor_copy(
+                    out=dst[:, 0 : 16 * vector_cols],
+                    in_=table[:].indirect(offsets[:, 0:vector_cols]),
+                )
+            nc.scalar.activation(
+                out=dst[:, 16 * vector_cols : J],
+                in_=table[:].indirect(offsets[:, vector_cols:LIST_COLS]),
+                func=ACT.Copy,
+            )
+
+        ra_all = ps.tile([P, PACK, P], F32, name="ra_all", tag="ra")
+        for s in range(PACK):
+            nc.tensor.transpose(ra_all[:, s, :], ra4[:, s : s + 1].to_broadcast([P, P]), ident[:])
+        bn_ps = ps.tile([P, HALVES, P], F32, name="bn_ps", tag="x2")
+        for a in range(HALVES):
+            nc.tensor.transpose(bn_ps[:, a, :], bn2[:, a : a + 1].to_broadcast([P, P]), ident[:])
+        bn_all = sb.tile([P, P, HALVES], F32, name="bn_all")
+        nc.scalar.copy(out=bn_all[:], in_=bn_ps[:].rearrange("r a p -> r p a"))
+
+        g_ps = []
+        g_max = []
+
+        def g_pick_and_measure(a):
+            g_pick = sb.tile([P, J], F32, name=f"g_pick{a}")
+            gather(g_pick, g_tab[a], g_list, G_SHARE[a])
+            bank = ps.tile([P, PACK, P], F32, name=f"g_ps{a}", tag=f"g{a}")
+            for s in range(PACK):
+                nc.tensor.transpose(bank[:, s, :], g_pick[:, s:J:PACK], ident[:])
+            g_abs = sb.tile([P, PACK, P], F32, name=f"g_abs{a}")
+            nc.scalar.activation(out=g_abs[:], in_=bank[:], func=ACT.Abs)
+            top = sb.tile([P, PACK], F32, name=f"g_max{a}")
+            nc.vector.tensor_reduce(out=top[:], in_=g_abs[:], axis=AXIS_X, op=ALU.max)
+            g_ps.append(bank)
+            g_max.append(top)
+
+        g_codes = sb.tile([P, N], U32, name="g_codes", align_bytes=64)
+        g_scales = sb.tile([P, N], U8, name="g_scales", align_bytes=64)
+
+        def g_quantise():
+            g_top = sb.tile([P, PACK], F32, name="g_top")
+            nc.vector.tensor_scalar(out=g_top[:], in0=g_max[0][:], scalar1=0.2, scalar2=None, op0=ALU.add)
+            g_den = sb.tile([P, PACK], F32, name="g_den")
+            nc.vector.scalar_tensor_tensor(
+                out=g_den[:], in0=g_max[1][:], scalar=0.2, in1=g_top[:], op0=ALU.add, op1=ALU.max
+            )
+            g_inv = sb.tile([P, PACK], F32, name="g_inv")
+            nc.vector.reciprocal(out=g_inv[:], in_=g_den[:])
+            g_fac = sb.tile([P, PACK], F32, name="g_fac")
+            nc.vector.tensor_tensor(out=g_fac[:], in0=g_inv[:], in1=cb4[:], op=ALU.mult)
+            g_bf = sb.tile([P, N, PACK], BF16, name="g_bf", align_bytes=64)
+            for a in range(HALVES):
+                nc.vector.tensor_tensor(
+                    out=g_bf[:, a * P : (a + 1) * P, :],
+                    in0=g_ps[a][:].rearrange("q s n -> q n s"),
+                    in1=g_fac[:].unsqueeze(1).to_broadcast([P, P, PACK]),
+                    op=ALU.mult,
+                )
+            nc.vector.quantize_mx(
+                out=g_codes[:].bitcast(E5M2X4), scales=g_scales[:], in_=g_bf[:].rearrange("q n s -> q (n s)")
+            )
+
+        x_quant = []
+
+        def x_quantise(t):
+            x_pick = sb.tile([P, J], F32, name=f"x_pick{t}")
+            gather(x_pick, x_tab[t], x_list, X_SHARE[t])
+            x_bf = sb.tile([P, J], BF16, name=f"x_bf{t}")
+            step = P // X_PARTS[t]
+            for q0 in range(0, P, step):
+                cols = slice(PACK * q0, PACK * (q0 + step))
+                nc.vector.scalar_tensor_tensor(
+                    out=x_bf[:, cols].rearrange("p (q s) -> p q s", s=PACK),
+                    in0=x_pick[:, cols].rearrange("p (q s) -> p q s", s=PACK),
+                    scalar=fk4[:, t : t + 1],
+                    in1=ra_all[:, :, q0 : q0 + step].rearrange("p s q -> p q s"),
+                    op0=ALU.mult,
+                    op1=ALU.mult,
+                )
+            pairs = x_bf[:].bitcast(F32)
+            x_ps = ps.tile([P, 2, P], F32, name=f"x_ps{t}", tag=f"x{t % 3}")
+            for u in range(2):
+                nc.tensor.transpose(x_ps[:, u, :], pairs[:, u : J // 2 : 2], ident[:])
+            x_in = sb.tile([P, P * PACK], BF16, name=f"x_in{t}", align_bytes=64)
+            nc.scalar.copy(
+                out=x_in[:].bitcast(F32).rearrange("q (m u) -> q m u", u=2),
+                in_=x_ps[:].rearrange("q u m -> q m u"),
+            )
+            x_codes = sb.tile([P, P], U32, name=f"x_codes{t}", align_bytes=64)
+            x_scales = sb.tile([P, P], U8, name=f"x_scales{t}", align_bytes=64)
+            nc.vector.quantize_mx(out=x_codes[:].bitcast(E5M2X4), scales=x_scales[:], in_=x_in[:])
+            x_quant.append((x_codes, x_scales))
+
+        g_pick_and_measure(0)
+        x_quantise(0)
+        g_pick_and_measure(1)
+        x_quantise(1)
+        g_quantise()
+        x_quantise(2)
+        x_quantise(3)
+
+        w_ps = [ps.tile([P, PACK, P], F32, name=f"w_ps{h}", tag=f"w{h}") for h in range(HALVES)]
+        for t in range(PACK):
+            for h in range(HALVES):
+                cols = slice(h * P, (h + 1) * P)
+                nc.tensor.matmul_mx(
+                    out=w_ps[h][:, t, :],
+                    lhsT=x_quant[t][0][:].bitcast(E5M2X4),
+                    lhsT_scale=x_quant[t][1][:],
+                    rhs=g_codes[:, cols].bitcast(E5M2X4),
+                    rhs_scale=g_scales[:, cols],
+                    start=True,
+                    stop=True,
+                )
+
+        w_codes = sb.tile([P, N], U32, name="w_codes", align_bytes=64)
+        w_scales = sb.tile([P, N], U8, name="w_scales", align_bytes=64)
+        w_bf = [sb.tile([P, P, PACK], BF16, name=f"w_bf{h}", align_bytes=64) for h in range(HALVES)]
+        nc.vector.tensor_copy(out=w_bf[0][:], in_=w_ps[0][:].rearrange("p t n -> p n t"))
+        nc.scalar.copy(out=w_bf[1][:], in_=w_ps[1][:].rearrange("p t n -> p n t"))
+        for h in range(HALVES):
+            cols = slice(h * P, (h + 1) * P)
+            nc.vector.quantize_mx(
+                out=w_codes[:, cols].bitcast(E5M2X4),
+                scales=w_scales[:, cols],
+                in_=w_bf[h][:].rearrange("p n t -> p (n t)"),
+            )
+
+        v_ps = [ps.tile([P, N], F32, name=f"v_ps{a}", tag=f"g{a}") for a in range(HALVES)]
+        for h in range(HALVES):
+            cols = slice(h * P, (h + 1) * P)
+            for a in range(HALVES):
+                nc.tensor.matmul_mx(
+                    out=v_ps[a][:, cols],
+                    lhsT=dr_w[:, 2 * a * P : 2 * (a + 1) * P].bitcast(E2M1X4),
+                    lhsT_scale=dr_s[:, a * P : (a + 1) * P],
+                    rhs=w_codes[:, cols].bitcast(E5M2X4),
+                    rhs_scale=w_scales[:, cols],
+                    start=True,
+                    stop=True,
+                )
+        stores = [nc.sync, nc.scalar]
+        for a in range(HALVES):
+            neg = sb.tile([P, N], F32, name=f"neg{a}")
+            neg_sum = sb.tile([P, 1], F32, name=f"neg_sum{a}")
+            nc.vector.scalar_tensor_tensor(
+                out=neg[:],
+                in0=v_ps[a][:],
+                scalar=-1.0,
+                in1=bn_all[:].rearrange("r p a -> r (p a)"),
+                op0=ALU.mult,
+                op1=ALU.subtract,
+                accum_out=neg_sum[:],
+            )
+            dev = sb.tile([P, N], F32, name=f"dev{a}")
+            dev_sum = sb.tile([P, 1], F32, name=f"dev_sum{a}")
+            nc.scalar.activation(
+                out=dev[:], in_=neg[:], func=ACT.Abs, bias=neg_sum[:], scale=-float(N), accum_out=dev_sum[:]
+            )
+            neg_mean = sb.tile([P, 1], F32, name=f"neg_mean{a}")
+            nc.vector.tensor_scalar(out=neg_mean[:], in0=neg_sum[:], scalar1=1.0 / N, scalar2=None, op0=ALU.mult)
+            neg_den = sb.tile([P, 1], F32, name=f"neg_den{a}")
+            nc.vector.tensor_scalar(
+                out=neg_den[:], in0=dev_sum[:], scalar1=-1.0 / (N * N), scalar2=2.0, op0=ALU.mult, op1=ALU.subtract
+            )
+            neg_inv = sb.tile([P, 1], F32, name=f"neg_inv{a}")
+            nc.vector.reciprocal(out=neg_inv[:], in_=neg_den[:])
+            res = sb.tile([P, N], F32, name=f"res{a}")
+            nc.vector.tensor_scalar(
+                out=res[:], in0=neg[:], scalar1=neg_mean[:], scalar2=neg_inv[:], op0=ALU.subtract, op1=ALU.mult
+            )
+            stores[a].dma_start(out=out[a * P : (a + 1) * P, :], in_=res[:])

@@ -22,9 +22,9 @@ P = 128
 PACK = 4
 HALVES = 2
 LIST_COLS = J // 16
-G_SHARE = [16, 18]
-X_SHARE = [16, 0, 0, 16]
-X_PARTS = [1, 1, 1, 2]
+G_SHARE = [16, 16]
+X_SHARE = [16, 0, 0, 0]
+X_GROUPS = [([0], "g0"), ([1], "g1"), ([2], "x2"), ([3], "x3")]
 
 
 def tile_list_directions_headpicks_sized_spread_kernel(
@@ -42,26 +42,29 @@ def tile_list_directions_headpicks_sized_spread_kernel(
         ra4 = sb.tile([P, PACK], F32, name="ra4")
         fk4 = sb.tile([P, PACK], F32, name="fk4")
         cb4 = sb.tile([P, PACK], F32, name="cb4")
-        bn2 = sb.tile([P, HALVES], F32, name="bn2")
+        bn_all = sb.tile([P, N], F32, name="bn_all")
         dr_w = sb.tile([P, 2 * R], U8, name="dr_w", align_bytes=64)
         dr_s = sb.tile([P, R], U8, name="dr_s", align_bytes=64)
         ident = sb.tile([P, P], F32, name="ident")
 
         x_rows = xf.rearrange("(p t) c -> t p c", t=PACK)
-        nc.sync.dma_start(out=g_tab[0][:], in_=gt[0:P, :])
         nc.sync.dma_start(g_list[:], offs2)
         nc.sync.dma_start(x_list[:], offs)
         nc.scalar.dma_start(out=ra4[:], in_=ra.rearrange("o (q s) -> q (o s)", s=PACK))
         nc.scalar.dma_start(out=fk4[:], in_=fkr.rearrange("o (p t) -> p (o t)", t=PACK))
-        nc.sync.dma_start(out=x_tab[0][:], in_=x_rows[0])
-        nc.sync.dma_start(out=g_tab[1][:], in_=gt[P : 2 * P, :])
-        nc.scalar.dma_start(out=bn2[:], in_=bn.rearrange("o (p a) -> p (o a)", a=HALVES))
-        for t in range(1, PACK):
+        nc.scalar.dma_start(out=cb4[:], in_=cb.rearrange("(q s) o -> q (s o)", s=PACK))
+        for a in range(HALVES):
+            nc.sync.dma_start(out=g_tab[a][:], in_=gt[a * P : (a + 1) * P, :])
+        for t in range(PACK):
             nc.sync.dma_start(out=x_tab[t][:], in_=x_rows[t])
-        nc.sync.dma_start(out=cb4[:], in_=cb.rearrange("(q s) o -> q (s o)", s=PACK))
         make_identity(nc, ident[:])
+        warm = sb.tile([P, 1], F32, name="warm")
+        warmed = sb.tile([P, 1], F32, name="warmed")
+        nc.vector.memset(warm[:], 0.0)
+        nc.scalar.activation(out=warmed[:], in_=warm[:], func=ACT.Abs)
         nc.gpsimd.memset(dr_s[:].bitcast(I32), 0)
         nc.sync.dma_start(out=dr_w[:].bitcast(I32), in_=dr_words[0].bitcast(I32))
+        nc.sync.dma_start(out=bn_all[:], in_=bn[0].partition_broadcast(P))
         for q in range(4):
             nc.sync.dma_start(
                 out=dr_s[32 * q : 32 * q + 4, :].bitcast(I32),
@@ -83,92 +86,99 @@ def tile_list_directions_headpicks_sized_spread_kernel(
         ra_all = ps.tile([P, PACK, P], F32, name="ra_all", tag="ra")
         for s in range(PACK):
             nc.tensor.transpose(ra_all[:, s, :], ra4[:, s : s + 1].to_broadcast([P, P]), ident[:])
-        bn_ps = ps.tile([P, HALVES, P], F32, name="bn_ps", tag="x2")
-        for a in range(HALVES):
-            nc.tensor.transpose(bn_ps[:, a, :], bn2[:, a : a + 1].to_broadcast([P, P]), ident[:])
-        bn_all = sb.tile([P, P, HALVES], F32, name="bn_all")
-        nc.scalar.copy(out=bn_all[:], in_=bn_ps[:].rearrange("r a p -> r p a"))
+
+        cb_inv = sb.tile([P, PACK], F32, name="cb_inv")
+        nc.vector.reciprocal(out=cb_inv[:], in_=cb4[:])
 
         g_ps = []
-        g_max = []
-
-        def g_pick_and_measure(a):
-            g_pick = sb.tile([P, J], F32, name=f"g_pick{a}")
+        g_abs = [sb.tile([P, PACK, P + a], F32, name=f"g_abs{a}", tag=f"abs{a}") for a in range(HALVES)]
+        g_top = sb.tile([P, PACK], F32, name="g_top")
+        g_max = [g_abs[1][:, :, P], g_top[:]]
+        for a in range(HALVES):
+            g_pick = sb.tile([P, J], F32, name=f"g_pick{a}", tag=f"pick{a}")
             gather(g_pick, g_tab[a], g_list, G_SHARE[a])
             bank = ps.tile([P, PACK, P], F32, name=f"g_ps{a}", tag=f"g{a}")
             for s in range(PACK):
                 nc.tensor.transpose(bank[:, s, :], g_pick[:, s:J:PACK], ident[:])
-            g_abs = sb.tile([P, PACK, P], F32, name=f"g_abs{a}")
-            nc.scalar.activation(out=g_abs[:], in_=bank[:], func=ACT.Abs)
-            top = sb.tile([P, PACK], F32, name=f"g_max{a}")
-            nc.vector.tensor_reduce(out=top[:], in_=g_abs[:], axis=AXIS_X, op=ALU.max)
             g_ps.append(bank)
-            g_max.append(top)
+
+        def g_magnitude(a):
+            nc.scalar.activation(out=g_abs[a][:, :, 0:P], in_=g_ps[a][:], func=ACT.Abs)
+
+        def g_largest(a):
+            nc.vector.tensor_reduce(out=g_max[a], in_=g_abs[a][:], axis=AXIS_X, op=ALU.max)
+
+        x_pick = []
+        x_bf = []
+
+        def x_gather(t, tag):
+            one = sb.tile([P, J], F32, name=f"x_pick{t}", tag=tag)
+            gather(one, x_tab[t], x_list, X_SHARE[t])
+            x_pick.append(one)
+
+        def x_weigh(t, tag):
+            one = sb.tile([P, J], BF16, name=f"x_bf{t}", tag=tag)
+            nc.vector.scalar_tensor_tensor(
+                out=one[:].rearrange("p (q s) -> p q s", s=PACK),
+                in0=x_pick[t][:].rearrange("p (q s) -> p q s", s=PACK),
+                scalar=fk4[:, t : t + 1],
+                in1=ra_all[:].rearrange("p s q -> p q s"),
+                op0=ALU.mult,
+                op1=ALU.mult,
+            )
+            x_bf.append(one)
+
+        g_magnitude(0)
+        g_largest(0)
+        x_gather(0, "pick0")
+        g_magnitude(1)
+        x_weigh(0, "x_bf0")
+        g_largest(1)
 
         g_codes = sb.tile([P, N], U32, name="g_codes", align_bytes=64)
         g_scales = sb.tile([P, N], U8, name="g_scales", align_bytes=64)
-
-        def g_quantise():
-            g_top = sb.tile([P, PACK], F32, name="g_top")
-            nc.vector.tensor_scalar(out=g_top[:], in0=g_max[0][:], scalar1=0.2, scalar2=None, op0=ALU.add)
-            g_den = sb.tile([P, PACK], F32, name="g_den")
-            nc.vector.scalar_tensor_tensor(
-                out=g_den[:], in0=g_max[1][:], scalar=0.2, in1=g_top[:], op0=ALU.add, op1=ALU.max
+        g_den = sb.tile([P, PACK], F32, name="g_den", tag="den")
+        nc.vector.scalar_tensor_tensor(
+            out=g_den[:], in0=g_top[:], scalar=0.2, in1=cb_inv[:], op0=ALU.add, op1=ALU.mult
+        )
+        g_fac = sb.tile([P, PACK], F32, name="g_fac")
+        nc.vector.reciprocal(out=g_fac[:], in_=g_den[:])
+        x_gather(1, "pick1")
+        x_weigh(1, "den")
+        g_bf = sb.tile([P, N, PACK], BF16, name="g_bf", align_bytes=64)
+        for a in range(HALVES):
+            nc.vector.tensor_tensor(
+                out=g_bf[:, a * P : (a + 1) * P, :],
+                in0=g_ps[a][:].rearrange("q s n -> q n s"),
+                in1=g_fac[:].unsqueeze(1).to_broadcast([P, P, PACK]),
+                op=ALU.mult,
             )
-            g_inv = sb.tile([P, PACK], F32, name="g_inv")
-            nc.vector.reciprocal(out=g_inv[:], in_=g_den[:])
-            g_fac = sb.tile([P, PACK], F32, name="g_fac")
-            nc.vector.tensor_tensor(out=g_fac[:], in0=g_inv[:], in1=cb4[:], op=ALU.mult)
-            g_bf = sb.tile([P, N, PACK], BF16, name="g_bf", align_bytes=64)
-            for a in range(HALVES):
-                nc.vector.tensor_tensor(
-                    out=g_bf[:, a * P : (a + 1) * P, :],
-                    in0=g_ps[a][:].rearrange("q s n -> q n s"),
-                    in1=g_fac[:].unsqueeze(1).to_broadcast([P, P, PACK]),
-                    op=ALU.mult,
-                )
-            nc.vector.quantize_mx(
-                out=g_codes[:].bitcast(E5M2X4), scales=g_scales[:], in_=g_bf[:].rearrange("q n s -> q (n s)")
-            )
+        x_gather(2, "pick0")
+        x_weigh(2, "pick1")
+        x_gather(3, "abs1")
+        x_weigh(3, "x_bf3")
+        nc.vector.quantize_mx(
+            out=g_codes[:].bitcast(E5M2X4), scales=g_scales[:], in_=g_bf[:].rearrange("q n s -> q (n s)")
+        )
 
         x_quant = []
-
-        def x_quantise(t):
-            x_pick = sb.tile([P, J], F32, name=f"x_pick{t}")
-            gather(x_pick, x_tab[t], x_list, X_SHARE[t])
-            x_bf = sb.tile([P, J], BF16, name=f"x_bf{t}")
-            step = P // X_PARTS[t]
-            for q0 in range(0, P, step):
-                cols = slice(PACK * q0, PACK * (q0 + step))
-                nc.vector.scalar_tensor_tensor(
-                    out=x_bf[:, cols].rearrange("p (q s) -> p q s", s=PACK),
-                    in0=x_pick[:, cols].rearrange("p (q s) -> p q s", s=PACK),
-                    scalar=fk4[:, t : t + 1],
-                    in1=ra_all[:, :, q0 : q0 + step].rearrange("p s q -> p q s"),
-                    op0=ALU.mult,
-                    op1=ALU.mult,
-                )
-            pairs = x_bf[:].bitcast(F32)
-            x_ps = ps.tile([P, 2, P], F32, name=f"x_ps{t}", tag=f"x{t % 3}")
-            for u in range(2):
-                nc.tensor.transpose(x_ps[:, u, :], pairs[:, u : J // 2 : 2], ident[:])
-            x_in = sb.tile([P, P * PACK], BF16, name=f"x_in{t}", align_bytes=64)
+        for tiles, tag in X_GROUPS:
+            count = len(tiles)
+            x_ps = ps.tile([P, count, 2, P], F32, name=f"x_ps{tiles[0]}", tag=tag)
+            for i, t in enumerate(tiles):
+                pairs = x_bf[t][:].bitcast(F32)
+                for u in range(2):
+                    nc.tensor.transpose(x_ps[:, i, u, :], pairs[:, u : J // 2 : 2], ident[:])
+            x_in = sb.tile([P, count * P * PACK], BF16, name=f"x_in{tiles[0]}", align_bytes=64)
             nc.scalar.copy(
-                out=x_in[:].bitcast(F32).rearrange("q (m u) -> q m u", u=2),
-                in_=x_ps[:].rearrange("q u m -> q m u"),
+                out=x_in[:].bitcast(F32).rearrange("q (i m u) -> q i m u", i=count, u=2),
+                in_=x_ps[:].rearrange("q i u m -> q i m u"),
             )
-            x_codes = sb.tile([P, P], U32, name=f"x_codes{t}", align_bytes=64)
-            x_scales = sb.tile([P, P], U8, name=f"x_scales{t}", align_bytes=64)
+            x_codes = sb.tile([P, count * P], U32, name=f"x_codes{tiles[0]}", align_bytes=64)
+            x_scales = sb.tile([P, count * P], U8, name=f"x_scales{tiles[0]}", align_bytes=64)
             nc.vector.quantize_mx(out=x_codes[:].bitcast(E5M2X4), scales=x_scales[:], in_=x_in[:])
-            x_quant.append((x_codes, x_scales))
-
-        g_pick_and_measure(0)
-        x_quantise(0)
-        g_pick_and_measure(1)
-        x_quantise(1)
-        g_quantise()
-        x_quantise(2)
-        x_quantise(3)
+            for i in range(count):
+                x_quant.append((x_codes[:, i * P : (i + 1) * P], x_scales[:, i * P : (i + 1) * P]))
 
         w_ps = [ps.tile([P, PACK, P], F32, name=f"w_ps{h}", tag=f"w{h}") for h in range(HALVES)]
         for t in range(PACK):
@@ -176,8 +186,8 @@ def tile_list_directions_headpicks_sized_spread_kernel(
                 cols = slice(h * P, (h + 1) * P)
                 nc.tensor.matmul_mx(
                     out=w_ps[h][:, t, :],
-                    lhsT=x_quant[t][0][:].bitcast(E5M2X4),
-                    lhsT_scale=x_quant[t][1][:],
+                    lhsT=x_quant[t][0].bitcast(E5M2X4),
+                    lhsT_scale=x_quant[t][1],
                     rhs=g_codes[:, cols].bitcast(E5M2X4),
                     rhs_scale=g_scales[:, cols],
                     start=True,
@@ -197,7 +207,7 @@ def tile_list_directions_headpicks_sized_spread_kernel(
                 in_=w_bf[h][:].rearrange("p n t -> p (n t)"),
             )
 
-        v_ps = [ps.tile([P, N], F32, name=f"v_ps{a}", tag=f"g{a}") for a in range(HALVES)]
+        v_ps = [ps.tile([P, N], F32, name=f"v_ps{a}", tag=["ra", "v1"][a]) for a in range(HALVES)]
         for h in range(HALVES):
             cols = slice(h * P, (h + 1) * P)
             for a in range(HALVES):
@@ -218,7 +228,7 @@ def tile_list_directions_headpicks_sized_spread_kernel(
                 out=neg[:],
                 in0=v_ps[a][:],
                 scalar=-1.0,
-                in1=bn_all[:].rearrange("r p a -> r (p a)"),
+                in1=bn_all[:],
                 op0=ALU.mult,
                 op1=ALU.subtract,
                 accum_out=neg_sum[:],

@@ -49,12 +49,12 @@ def tile_list_directions_headpicks_sized_spread_kernel(
 
         x_rows = xf.rearrange("(p t) c -> t p c", t=PACK)
         nc.sync.dma_start(g_list[:], offs2)
+        nc.scalar.dma_start(out=g_tab[0][:], in_=gt[0:P, :])
+        nc.sync.dma_start(out=ra4[:], in_=ra.rearrange("o (q s) -> q (o s)", s=PACK))
         nc.sync.dma_start(x_list[:], offs)
-        nc.scalar.dma_start(out=ra4[:], in_=ra.rearrange("o (q s) -> q (o s)", s=PACK))
-        nc.scalar.dma_start(out=fk4[:], in_=fkr.rearrange("o (p t) -> p (o t)", t=PACK))
-        nc.scalar.dma_start(out=cb4[:], in_=cb.rearrange("(q s) o -> q (s o)", s=PACK))
-        for a in range(HALVES):
-            nc.sync.dma_start(out=g_tab[a][:], in_=gt[a * P : (a + 1) * P, :])
+        nc.sync.dma_start(out=fk4[:], in_=fkr.rearrange("o (p t) -> p (o t)", t=PACK))
+        nc.sync.dma_start(out=cb4[:], in_=cb.rearrange("(q s) o -> q (s o)", s=PACK))
+        nc.sync.dma_start(out=g_tab[1][:], in_=gt[P : 2 * P, :])
         for t in range(PACK):
             nc.sync.dma_start(out=x_tab[t][:], in_=x_rows[t])
         make_identity(nc, ident[:])

@@ -58,10 +58,6 @@ def tile_list_directions_headpicks_sized_spread_kernel(
         for t in range(PACK):
             nc.sync.dma_start(out=x_tab[t][:], in_=x_rows[t])
         make_identity(nc, ident[:])
-        warm = sb.tile([P, 1], F32, name="warm")
-        warmed = sb.tile([P, 1], F32, name="warmed")
-        nc.vector.memset(warm[:], 0.0)
-        nc.scalar.activation(out=warmed[:], in_=warm[:], func=ACT.Abs)
         nc.gpsimd.memset(dr_s[:].bitcast(I32), 0)
         nc.sync.dma_start(out=dr_w[:].bitcast(I32), in_=dr_words[0].bitcast(I32))
         nc.sync.dma_start(out=bn_all[:], in_=bn[0].partition_broadcast(P))

from contextlib import ExitStack

import concourse.mybir as mybir
from concourse.masks import make_identity

K, J, N, R, T, V = 512, 512, 256, 256, 1024, 1024
FLOPS = 2 * J * K * N + 2 * K * R * N

F32 = mybir.dt.float32
BF16 = mybir.dt.bfloat16
I32 = mybir.dt.int32
U32 = mybir.dt.uint32
U16 = mybir.dt.uint16
U8 = mybir.dt.uint8
E5M2X4 = mybir.dt.float8_e5m2_x4
E2M1X4 = mybir.dt.float4_e2m1fn_x4
ALU = mybir.AluOpType
ACT = mybir.ActivationFunctionType
AXIS_X = mybir.AxisListType.X

P = 128
PACK = 4
HALVES = 2
LIST_COLS = J // 16
G_SHARE = [16, 16]
X_SHARE = [16, 0, 0, 0]
X_GROUPS = [([0], "g0"), ([1], "g1"), ([2], "x2"), ([3], "x3")]


def tile_list_directions_headpicks_sized_spread_kernel(
    tc, xf, ra, gt, cb, fkr, dr_words, dr_scales, bn, offs, offs2, out
):
    nc = tc.nc
    with ExitStack() as ctx:
        sb = ctx.enter_context(tc.tile_pool(name="sb", bufs=1))
        ps = ctx.enter_context(tc.psum_pool(name="ps", bufs=1))

        x_list = sb.tile([P, LIST_COLS], U16, name="x_list")
        g_list = sb.tile([P, LIST_COLS], U16, name="g_list")
        g_tab = [sb.tile([P, V], F32, name=f"g_tab{a}") for a in range(HALVES)]
        x_tab = [sb.tile([P, T], F32, name=f"x_tab{t}") for t in range(PACK)]
        ra4 = sb.tile([P, PACK], F32, name="ra4")
        fk4 = sb.tile([P, PACK], F32, name="fk4")
        cb4 = sb.tile([P, PACK], F32, name="cb4")
        bn_all = sb.tile([P, N], F32, name="bn_all")
        dr_w = sb.tile([P, 2 * R], U8, name="dr_w", align_bytes=64)
        dr_s = sb.tile([P, R], U8, name="dr_s", align_bytes=64)
        ident = sb.tile([P, P], F32, name="ident")

        x_rows = xf.rearrange("(p t) c -> t p c", t=PACK)
        nc.sync.dma_start(g_list[:], offs2)
        nc.scalar.dma_start(out=g_tab[0][:], in_=gt[0:P, :])
        nc.sync.dma_start(out=ra4[:], in_=ra.rearrange("o (q s) -> q (o s)", s=PACK))
        nc.sync.dma_start(x_list[:], offs)
        nc.sync.dma_start(out=fk4[:], in_=fkr.rearrange("o (p t) -> p (o t)", t=PACK))
        nc.sync.dma_start(out=cb4[:], in_=cb.rearrange("(q s) o -> q (s o)", s=PACK))
        nc.sync.dma_start(out=g_tab[1][:], in_=gt[P : 2 * P, :])
        for t in range(PACK):
            nc.sync.dma_start(out=x_tab[t][:], in_=x_rows[t])
        make_identity(nc, ident[:])
        nc.gpsimd.memset(dr_s[:].bitcast(I32), 0)
        nc.sync.dma_start(out=dr_w[:].bitcast(I32), in_=dr_words[0].bitcast(I32))
        nc.sync.dma_start(out=bn_all[:], in_=bn[0].partition_broadcast(P))
        for q in range(4):
            nc.sync.dma_start(
                out=dr_s[32 * q : 32 * q + 4, :].bitcast(I32),
                in_=dr_scales[0, 4 * q : 4 * q + 4, :].bitcast(I32),
            )

        def gather(dst, table, offsets, vector_cols):
            if vector_cols > 0:
                nc.vector.tensor_copy(
                    out=dst[:, 0 : 16 * vector_cols],
                    in_=table[:].indirect(offsets[:, 0:vector_cols]),
                )
            nc.scalar.activation(
                out=dst[:, 16 * vector_cols : J],
                in_=table[:].indirect(offsets[:, vector_cols:LIST_COLS]),
                func=ACT.Copy,
            )

        ra_all = ps.tile([P, PACK, P], F32, name="ra_all", tag="ra")
        for s in range(PACK):
            nc.tensor.transpose(ra_all[:, s, :], ra4[:, s : s + 1].to_broadcast([P, P]), ident[:])

        cb_inv = sb.tile([P, PACK], F32, name="cb_inv")
        nc.vector.reciprocal(out=cb_inv[:], in_=cb4[:])

        g_ps = []
        g_abs = [sb.tile([P, PACK, P + a], F32, name=f"g_abs{a}", tag=f"abs{a}") for a in range(HALVES)]
        g_top = sb.tile([P, PACK], F32, name="g_top")
        g_max = [g_abs[1][:, :, P], g_top[:]]
        for a in range(HALVES):
            g_pick = sb.tile([P, J], F32, name=f"g_pick{a}", tag=f"pick{a}")
            gather(g_pick, g_tab[a], g_list, G_SHARE[a])
            bank = ps.tile([P, PACK, P], F32, name=f"g_ps{a}", tag=f"g{a}")
            for s in range(PACK):
                nc.tensor.transpose(bank[:, s, :], g_pick[:, s:J:PACK], ident[:])
            g_ps.append(bank)

        def g_magnitude(a):
            nc.scalar.activation(out=g_abs[a][:, :, 0:P], in_=g_ps[a][:], func=ACT.Abs)

        def g_largest(a):
            nc.vector.tensor_reduce(out=g_max[a], in_=g_abs[a][:], axis=AXIS_X, op=ALU.max)

        x_pick = []
        x_bf = []

        def x_gather(t, tag):
            one = sb.tile([P, J], F32, name=f"x_pick{t}", tag=tag)
            gather(one, x_tab[t], x_list, X_SHARE[t])
            x_pick.append(one)

        def x_weigh(t, tag):
            one = sb.tile([P, J], BF16, name=f"x_bf{t}", tag=tag)
            nc.vector.scalar_tensor_tensor(
                out=one[:].rearrange("p (q s) -> p q s", s=PACK),
                in0=x_pick[t][:].rearrange("p (q s) -> p q s", s=PACK),
                scalar=fk4[:, t : t + 1],
                in1=ra_all[:].rearrange("p s q -> p q s"),
                op0=ALU.mult,
                op1=ALU.mult,
            )
            x_bf.append(one)

        g_magnitude(0)
        g_largest(0)
        x_gather(0, "pick0")
        g_magnitude(1)
        x_weigh(0, "x_bf0")
        g_largest(1)

        g_codes = sb.tile([P, N], U32, name="g_codes", align_bytes=64)
        g_scales = sb.tile([P, N], U8, name="g_scales", align_bytes=64)
        g_den = sb.tile([P, PACK], F32, name="g_den", tag="den")
        nc.vector.scalar_tensor_tensor(
            out=g_den[:], in0=g_top[:], scalar=0.2, in1=cb_inv[:], op0=ALU.add, op1=ALU.mult
        )
        g_fac = sb.tile([P, PACK], F32, name="g_fac")
        nc.vector.reciprocal(out=g_fac[:], in_=g_den[:])
        x_gather(1, "pick1")
        x_weigh(1, "den")
        g_bf = sb.tile([P, N, PACK], BF16, name="g_bf", align_bytes=64)
        for a in range(HALVES):
            nc.vector.tensor_tensor(
                out=g_bf[:, a * P : (a + 1) * P, :],
                in0=g_ps[a][:].rearrange("q s n -> q n s"),
                in1=g_fac[:].unsqueeze(1).to_broadcast([P, P, PACK]),
                op=ALU.mult,
            )
        x_gather(2, "pick0")
        x_weigh(2, "pick1")
        x_gather(3, "abs1")
        x_weigh(3, "x_bf3")
        nc.vector.quantize_mx(
            out=g_codes[:].bitcast(E5M2X4), scales=g_scales[:], in_=g_bf[:].rearrange("q n s -> q (n s)")
        )

        x_quant = []
        for tiles, tag in X_GROUPS:
            count = len(tiles)
            x_ps = ps.tile([P, count, 2, P], F32, name=f"x_ps{tiles[0]}", tag=tag)
            for i, t in enumerate(tiles):
                pairs = x_bf[t][:].bitcast(F32)
                for u in range(2):
                    nc.tensor.transpose(x_ps[:, i, u, :], pairs[:, u : J // 2 : 2], ident[:])
            x_in = sb.tile([P, count * P * PACK], BF16, name=f"x_in{tiles[0]}", align_bytes=64)
            nc.scalar.copy(
                out=x_in[:].bitcast(F32).rearrange("q (i m u) -> q i m u", i=count, u=2),
                in_=x_ps[:].rearrange("q i u m -> q i m u"),
            )
            x_codes = sb.tile([P, count * P], U32, name=f"x_codes{tiles[0]}", align_bytes=64)
            x_scales = sb.tile([P, count * P], U8, name=f"x_scales{tiles[0]}", align_bytes=64)
            nc.vector.quantize_mx(out=x_codes[:].bitcast(E5M2X4), scales=x_scales[:], in_=x_in[:])
            for i in range(count):
                x_quant.append((x_codes[:, i * P : (i + 1) * P], x_scales[:, i * P : (i + 1) * P]))

        w_ps = [ps.tile([P, PACK, P], F32, name=f"w_ps{h}", tag=f"w{h}") for h in range(HALVES)]
        for t in range(PACK):
            for h in range(HALVES):
                cols = slice(h * P, (h + 1) * P)
                nc.tensor.matmul_mx(
                    out=w_ps[h][:, t, :],
                    lhsT=x_quant[t][0].bitcast(E5M2X4),
                    lhsT_scale=x_quant[t][1],
                    rhs=g_codes[:, cols].bitcast(E5M2X4),
                    rhs_scale=g_scales[:, cols],
                    start=True,
                    stop=True,
                )

        w_codes = sb.tile([P, N], U32, name="w_codes", align_bytes=64)
        w_scales = sb.tile([P, N], U8, name="w_scales", align_bytes=64)
        w_bf = [sb.tile([P, P, PACK], BF16, name=f"w_bf{h}", align_bytes=64) for h in range(HALVES)]
        nc.vector.tensor_copy(out=w_bf[0][:], in_=w_ps[0][:].rearrange("p t n -> p n t"))
        nc.scalar.copy(out=w_bf[1][:], in_=w_ps[1][:].rearrange("p t n -> p n t"))
        for h in range(HALVES):
            cols = slice(h * P, (h + 1) * P)
            nc.vector.quantize_mx(
                out=w_codes[:, cols].bitcast(E5M2X4),
                scales=w_scales[:, cols],
                in_=w_bf[h][:].rearrange("p n t -> p (n t)"),
            )

        v_ps = [ps.tile([P, N], F32, name=f"v_ps{a}", tag=["ra", "v1"][a]) for a in range(HALVES)]
        for h in range(HALVES):
            cols = slice(h * P, (h + 1) * P)
            for a in range(HALVES):
                nc.tensor.matmul_mx(
                    out=v_ps[a][:, cols],
                    lhsT=dr_w[:, 2 * a * P : 2 * (a + 1) * P].bitcast(E2M1X4),
                    lhsT_scale=dr_s[:, a * P : (a + 1) * P],
                    rhs=w_codes[:, cols].bitcast(E5M2X4),
                    rhs_scale=w_scales[:, cols],
                    start=True,
                    stop=True,
                )
        stores = [nc.sync, nc.scalar]
        for a in range(HALVES):
            neg = sb.tile([P, N], F32, name=f"neg{a}")
            neg_sum = sb.tile([P, 1], F32, name=f"neg_sum{a}")
            nc.vector.scalar_tensor_tensor(
                out=neg[:],
                in0=v_ps[a][:],
                scalar=-1.0,
                in1=bn_all[:],
                op0=ALU.mult,
                op1=ALU.subtract,
                accum_out=neg_sum[:],
            )
            dev = sb.tile([P, N], F32, name=f"dev{a}")
            dev_sum = sb.tile([P, 1], F32, name=f"dev_sum{a}")
            nc.scalar.activation(
                out=dev[:], in_=neg[:], func=ACT.Abs, bias=neg_sum[:], scale=-float(N), accum_out=dev_sum[:]
            )
            neg_mean = sb.tile([P, 1], F32, name=f"neg_mean{a}")
            nc.vector.tensor_scalar(out=neg_mean[:], in0=neg_sum[:], scalar1=1.0 / N, scalar2=None, op0=ALU.mult)
            neg_den = sb.tile([P, 1], F32, name=f"neg_den{a}")
            nc.vector.tensor_scalar(
                out=neg_den[:], in0=dev_sum[:], scalar1=-1.0 / (N * N), scalar2=2.0, op0=ALU.mult, op1=ALU.subtract
            )
            neg_inv = sb.tile([P, 1], F32, name=f"neg_inv{a}")
            nc.vector.reciprocal(out=neg_inv[:], in_=neg_den[:])
            res = sb.tile([P, N], F32, name=f"res{a}")
            nc.vector.tensor_scalar(
                out=res[:], in0=neg[:], scalar1=neg_mean[:], scalar2=neg_inv[:], op0=ALU.subtract, op1=ALU.mult
            )
            stores[a].dma_start(out=out[a * P : (a + 1) * P, :], in_=res[:])
